import numpy as np
import ml_dtypes


def mxq(x, axis, fmt="e4m3"):
    dtype, down = {"e4m3": (ml_dtypes.float8_e4m3fn, 7), "e5m2": (ml_dtypes.float8_e5m2, 14)}[fmt]
    v = np.moveaxis(np.asarray(x, np.float32).astype(ml_dtypes.bfloat16).astype(np.float64), axis, -1)
    blocks = v.reshape(v.shape[:-1] + (-1, 32))
    amax = np.abs(blocks).max(-1, keepdims=True)
    byte = np.maximum(np.where(amax > 0, np.frexp(amax)[1] - 1 + 127, 0) - down, 1)
    scale = np.exp2(byte - 127.0)
    codes = (blocks / scale).astype(np.float32).astype(dtype).astype(np.float64)
    return np.moveaxis((codes * scale).reshape(v.shape), -1, axis)


WIDE = False


def mx_kscale(k):
    if not WIDE:
        return np.ones(k)
    levels = np.array([10, -10, 5, -5, 0])
    if k % 512:
        return np.exp2(np.random.permutation(np.resize(levels, k // 32))).repeat(32)
    a = np.empty((k // 512, 16))
    for p in range(k // 512):
        a[p, :8] = np.random.permutation(np.resize(levels, 8))
        for g in range(8):
            far = levels[np.abs(levels - a[p, g]) >= 10]
            a[p, g + 8] = far[np.random.randint(len(far))]
    return np.exp2(a.ravel()).repeat(32)


def f64(x):
    return np.asarray(x).astype(np.float64)


def striped(idx):
    return np.tile(idx.reshape(-1, 16).T, (8, 1)).astype(np.uint16)


def unstriped(offs):
    return offs[:16].T.reshape(-1).astype(np.int64)


def pack_weight(w):
    k, n = w.shape
    w = f64(np.asarray(w, np.float32).astype(ml_dtypes.bfloat16)).reshape(k // 32, 32, n)
    amax = np.abs(w).max(1)
    byte = np.clip(np.where(amax > 0, np.frexp(amax)[1] - 1 + 127 - 7, 1), 1, 254)
    scaled = (w * np.exp2(127.0 - byte)[:, None, :]).reshape(k, n).astype(np.float32)
    words = np.ascontiguousarray(scaled.reshape(k // 512, 128, 4, n).transpose(0, 1, 3, 2)).astype(ml_dtypes.float8_e4m3fn).view(np.uint8)
    return words, np.ascontiguousarray(byte.astype(np.uint8).reshape(k // 512, 16, n))


def unpack_weight(words, scales):
    g, p, n, _ = words.shape
    vals = np.ascontiguousarray(words).view(ml_dtypes.float8_e4m3fn).astype(np.float64) * np.repeat(np.exp2(scales.astype(np.float64) - 127.0), 8, axis=1)[..., None]
    return vals.transpose(0, 1, 3, 2).reshape(g * 512, n)


K, T, S, N, U, R = 1024, 1024, 512, 128, 1024, 256


def setup_inputs():
    n = np.random.standard_normal
    s = mx_kscale(K)[:, None]
    packed_xT = pack_weight(n((K, T)) * s)
    return {
        "x_words": packed_xT[0],
        "x_scales": packed_xT[1],
        "w1": (n((K, N)) / np.sqrt(K) / s).astype(np.float32),
        "lev": (n((N, U))).astype(np.float32),
        "tre": (0.4 * n((N, U))).astype(np.float32),
        "seas": (np.random.uniform(0.6, 1.5, (N, R))).astype(np.float32),
        "alpha": (np.random.uniform(0.2, 0.6, (N, 1))).astype(np.float32),
        "offs": striped(np.random.permutation(T)[:S]),
        "ser": striped(np.random.permutation(U)[:S]),
        "sea": striped(np.random.permutation(np.concatenate([np.arange(R), np.random.randint(0, R, S - R)]))),
    }


def reference(x_words, x_scales, w1, lev, tre, seas, alpha, offs, ser, sea):
    levg = f64(lev)[:, unstriped(ser)]
    treg = f64(tre)[:, unstriped(ser)]
    pred = levg + 0.9 * treg
    xq = unpack_weight(x_words, x_scales)[:, unstriped(offs)]
    y = mxq(f64(w1), 0, "e4m3").T @ xq
    sf = f64(seas)[:, unstriped(sea)]
    err = y / sf - pred
    lnew = pred + f64(alpha) * err
    tnew = 0.9 * treg + 0.2 * (f64(alpha) * err)
    return (lnew + 1.7 * tnew) * sf - np.abs(err)

@@ -1,0 +1,127 @@
+from contextlib import ExitStack
+
+import concourse.mybir as mybir
+
+K, T, S, M, U, R = 1024, 1024, 512, 128, 1024, 256
+FLOPS = 2 * K * M * S
+
+F32 = mybir.dt.float32
+BF16 = mybir.dt.bfloat16
+I32 = mybir.dt.int32
+U32 = mybir.dt.uint32
+U16 = mybir.dt.uint16
+U8 = mybir.dt.uint8
+FP8X4 = mybir.dt.float8_e4m3fn_x4
+ACT = mybir.ActivationFunctionType
+ALU = mybir.AluOpType
+
+P = 128
+PACK = 4
+K_PASS = P * PACK
+PASSES = K // K_PASS
+SEAS_WINDOW = 704
+HALVES = 2
+HALF = S // HALVES
+
+
+def tile_picked_yholtw_fc_p_kernel(tc, x_words, x_scales, w1, lev, tre, seas, alpha, offs, ser, sea, out):
+    nc = tc.nc
+    with ExitStack() as ctx:
+        keep = ctx.enter_context(tc.tile_pool(name="keep", bufs=1))
+        psum = ctx.enter_context(tc.psum_pool(name="psum", bufs=1))
+
+        sea_list = keep.tile([P, S // 16], U16, name="sea_list")
+        ser_list = keep.tile([P, S // 16], U16, name="ser_list")
+        obs_list = keep.tile([P, S // 16], U16, name="obs_list")
+        seas_win = keep.tile([P, SEAS_WINDOW], F32, name="seas_win")
+        lev_win = keep.tile([P, U], F32, name="lev_win")
+        tre_win = keep.tile([P, U], F32, name="tre_win")
+        word_win = [keep.tile([P, T], I32, name="word_win%d" % o) for o in range(PASSES)]
+        scale_win = keep.tile([P, T], U8, name="scale_win")
+        w_raw = [keep.tile([P, PACK, M], F32, name="w_raw%d" % o) for o in range(PASSES)]
+        alpha_col = keep.tile([P, 1], F32, name="alpha_col")
+
+        nc.vector.memset(scale_win[:].bitcast(I32), 0)
+        nc.vector.memset(seas_win[:, R:], 0.0)
+
+        nc.sync.dma_start(sea_list[:], sea)
+        nc.sync.dma_start(seas_win[:, :R], seas)
+        nc.sync.dma_start(ser_list[:], ser)
+        nc.sync.dma_start(lev_win[:], lev)
+        nc.sync.dma_start(tre_win[:], tre)
+        nc.sync.dma_start(obs_list[:], offs)
+        nc.sync.dma_start(word_win[0][:], x_words[0].rearrange("p c r -> p (c r)").bitcast(I32))
+        for q in range(4):
+            nc.sync.dma_start(scale_win[32 * q : 32 * q + 4 * PASSES, :].bitcast(I32),
+                              x_scales[:, 4 * q : 4 * q + 4, :].bitcast(I32))
+        for o in range(PASSES):
+            nc.sync.dma_start(w_raw[o][:], w1[o * K_PASS : (o + 1) * K_PASS, :].rearrange("(p j) m -> p j m", j=PACK))
+        nc.sync.dma_start(word_win[1][:], x_words[1].rearrange("p c r -> p (c r)").bitcast(I32))
+        nc.gpsimd.dma_start(alpha_col[:], alpha)
+
+        sf = keep.tile([P, S], F32, name="sf")
+        nc.vector.tensor_copy(sf[:], seas_win[:].indirect(sea_list[:]))
+        lev_sf = keep.tile([P, S], F32, name="lev_sf")
+        nc.vector.tensor_tensor(lev_sf[:], lev_win[:].indirect(ser_list[:]), sf[:], ALU.mult)
+        tre_sf = keep.tile([P, S], F32, name="tre_sf")
+        nc.vector.tensor_tensor(tre_sf[:], tre_win[:].indirect(ser_list[:]), sf[:], ALU.mult)
+
+        inv_root = keep.tile([P, S], F32, name="inv_root")
+        nc.scalar.activation(inv_root[:], sf[:], ACT.Abs_reciprocal_sqrt)
+        inv_abs = keep.tile([P, S], F32, name="inv_abs")
+        nc.scalar.activation(inv_abs[:], inv_root[:], ACT.Square)
+
+        x_codes = [keep.tile([P, S], U32, name="x_codes%d" % o, align_bytes=64) for o in range(PASSES)]
+        nc.vector.tensor_copy(x_codes[0][:], word_win[0][:].bitcast(U32).indirect(obs_list[:]))
+        x_scale = keep.tile([P, S], U8, name="x_scale", align_bytes=64)
+        nc.vector.tensor_copy(x_scale[:], scale_win[:].indirect(obs_list[:]))
+
+        w_bf = keep.tile([P, PASSES, M, PACK], BF16, name="w_bf", align_bytes=64)
+        for o in range(PASSES):
+            nc.scalar.copy(w_bf[:, o, :, :], w_raw[o][:].rearrange("p j m -> p m j"))
+        w_codes = keep.tile([P, PASSES * M], U32, name="w_codes", align_bytes=64)
+        w_scale = keep.tile([P, PASSES * M], U8, name="w_scale", align_bytes=64)
+        nc.vector.quantize_mx(out=w_codes[:].bitcast(FP8X4), scales=w_scale[:],
+                              in_=w_bf[:].rearrange("p o m j -> p (o m j)"))
+
+        cols = [slice(h * HALF, (h + 1) * HALF) for h in range(HALVES)]
+        for h in range(HALVES):
+            nc.vector.tensor_copy(x_codes[1][:, cols[h]],
+                                  word_win[1][:].bitcast(U32).indirect(obs_list[:, h * HALF // 16 : (h + 1) * HALF // 16]))
+
+        gain = keep.tile([P, 1], F32, name="gain")
+        nc.scalar.mul(gain[:], alpha_col[:], 1.0 + 1.7 * 0.2)
+
+        pred_sf = keep.tile([P, S], F32, name="pred_sf")
+        nc.vector.scalar_tensor_tensor(pred_sf[:], tre_sf[:], 0.9, lev_sf[:], ALU.mult, ALU.add)
+        base = keep.tile([P, S], F32, name="base")
+        nc.vector.scalar_tensor_tensor(base[:], tre_sf[:], 0.9 + 1.7 * 0.9, lev_sf[:], ALU.mult, ALU.add)
+
+        y = [psum.tile([P, HALF], F32, name="y%d" % h) for h in range(HALVES)]
+        for o in range(PASSES):
+            for h in range(HALVES):
+                nc.tensor.matmul_mx(
+                    out=y[h][:],
+                    lhsT=w_codes[:, o * M : (o + 1) * M].bitcast(FP8X4),
+                    lhsT_scale=w_scale[:, o * M : (o + 1) * M],
+                    rhs=x_codes[o][:, cols[h]].bitcast(FP8X4),
+                    rhs_scale=x_scale[4 * o :, cols[h]],
+                    start=(o == 0),
+                    stop=(o == PASSES - 1),
+                )
+
+        miss = [keep.tile([P, HALF], F32, name="miss%d" % h) for h in range(HALVES)]
+        size = [keep.tile([P, HALF], F32, name="size%d" % h) for h in range(HALVES)]
+        fore = [keep.tile([P, HALF], F32, name="fore%d" % h) for h in range(HALVES)]
+        abs_err = [keep.tile([P, HALF], F32, name="abs_err%d" % h) for h in range(HALVES)]
+        result = [keep.tile([P, HALF], F32, name="result%d" % h) for h in range(HALVES)]
+        for h in range(HALVES):
+            nc.vector.tensor_tensor(miss[h][:], y[h][:], pred_sf[:, cols[h]], ALU.subtract)
+            nc.scalar.activation(size[h][:], miss[h][:], ACT.Abs)
+        for h in range(HALVES):
+            nc.vector.scalar_tensor_tensor(fore[h][:], miss[h][:], gain[:], base[:, cols[h]], ALU.mult, ALU.add)
+        for h in range(HALVES):
+            nc.vector.tensor_tensor(abs_err[h][:], size[h][:], inv_abs[:, cols[h]], ALU.mult)
+        for h in range(HALVES):
+            nc.vector.tensor_tensor(result[h][:], fore[h][:], abs_err[h][:], ALU.subtract)
+            nc.sync.dma_start(out[:, cols[h]], result[h][:])

@@ -20,6 +20,7 @@ PACK = 4
 K_PASS = P * PACK
 PASSES = K // K_PASS
 SEAS_WINDOW = 704
+GAIN = 1.0 + 1.7 * 0.2
 HALVES = 2
 HALF = S // HALVES
 
@@ -38,7 +39,7 @@ def tile_picked_yholtw_fc_p_kernel(tc, x_words, x_scales, w1, lev, tre, seas, al
         tre_win = keep.tile([P, U], F32, name="tre_win")
         word_win = [keep.tile([P, T], I32, name="word_win%d" % o) for o in range(PASSES)]
         scale_win = keep.tile([P, T], U8, name="scale_win")
-        w_raw = [keep.tile([P, PACK, M], F32, name="w_raw%d" % o) for o in range(PASSES)]
+        w_raw = [keep.tile([P, PACK, M], F32, name="w_raw%d" % o, tag="w_raw%d" % o) for o in range(PASSES)]
         alpha_col = keep.tile([P, 1], F32, name="alpha_col")
 
         nc.vector.memset(scale_win[:].bitcast(I32), 0)
@@ -49,6 +50,7 @@ def tile_picked_yholtw_fc_p_kernel(tc, x_words, x_scales, w1, lev, tre, seas, al
         nc.sync.dma_start(ser_list[:], ser)
         nc.sync.dma_start(lev_win[:], lev)
         nc.sync.dma_start(tre_win[:], tre)
+        nc.sync.dma_start(alpha_col[:], alpha)
         nc.sync.dma_start(obs_list[:], offs)
         nc.sync.dma_start(word_win[0][:], x_words[0].rearrange("p c r -> p (c r)").bitcast(I32))
         for q in range(4):
@@ -57,17 +59,29 @@ def tile_picked_yholtw_fc_p_kernel(tc, x_words, x_scales, w1, lev, tre, seas, al
         for o in range(PASSES):
             nc.sync.dma_start(w_raw[o][:], w1[o * K_PASS : (o + 1) * K_PASS, :].rearrange("(p j) m -> p j m", j=PACK))
         nc.sync.dma_start(word_win[1][:], x_words[1].rearrange("p c r -> p (c r)").bitcast(I32))
-        nc.gpsimd.dma_start(alpha_col[:], alpha)
 
         sf = keep.tile([P, S], F32, name="sf")
         nc.vector.tensor_copy(sf[:], seas_win[:].indirect(sea_list[:]))
-        lev_sf = keep.tile([P, S], F32, name="lev_sf")
-        nc.vector.tensor_tensor(lev_sf[:], lev_win[:].indirect(ser_list[:]), sf[:], ALU.mult)
-        tre_sf = keep.tile([P, S], F32, name="tre_sf")
-        nc.vector.tensor_tensor(tre_sf[:], tre_win[:].indirect(ser_list[:]), sf[:], ALU.mult)
+        lev_g = keep.tile([P, S], F32, name="lev_g")
+        nc.vector.tensor_copy(lev_g[:], lev_win[:].indirect(ser_list[:]))
+        tre_g = keep.tile([P, S], F32, name="tre_g")
+        nc.vector.tensor_copy(tre_g[:], tre_win[:].indirect(ser_list[:]))
+
+        gain = keep.tile([P, 1], F32, name="gain")
+        lev_gain = keep.tile([P, 1], F32, name="lev_gain")
+        tre_gain = keep.tile([P, 1], F32, name="tre_gain")
+        nc.gpsimd.tensor_scalar(gain[:], alpha_col[:], GAIN, 0.0, ALU.mult, ALU.add)
+        nc.gpsimd.tensor_scalar(lev_gain[:], alpha_col[:], -GAIN, 1.0, ALU.mult, ALU.add)
+        nc.gpsimd.tensor_scalar(tre_gain[:], alpha_col[:], -GAIN, 1.0 + 1.7, ALU.mult, ALU.add)
 
         inv_root = keep.tile([P, S], F32, name="inv_root")
         nc.scalar.activation(inv_root[:], sf[:], ACT.Abs_reciprocal_sqrt)
+        damped_sf = keep.tile([P, S], F32, name="damped_sf")
+        nc.scalar.mul(damped_sf[:], sf[:], 0.9)
+        lev_sf = keep.tile([P, S], F32, name="lev_sf")
+        nc.gpsimd.tensor_tensor(lev_sf[:], lev_g[:], sf[:], ALU.mult)
+        tre_sf = keep.tile([P, S], F32, name="tre_sf")
+        nc.gpsimd.tensor_tensor(tre_sf[:], tre_g[:], damped_sf[:], ALU.mult)
         inv_abs = keep.tile([P, S], F32, name="inv_abs")
         nc.scalar.activation(inv_abs[:], inv_root[:], ACT.Square)
 
@@ -79,6 +93,11 @@ def tile_picked_yholtw_fc_p_kernel(tc, x_words, x_scales, w1, lev, tre, seas, al
         w_bf = keep.tile([P, PASSES, M, PACK], BF16, name="w_bf", align_bytes=64)
         for o in range(PASSES):
             nc.scalar.copy(w_bf[:, o, :, :], w_raw[o][:].rearrange("p j m -> p m j"))
+        parts = keep.tile([P, 2 * S], F32, name="parts", tag="w_raw1")
+        lev_part = parts[:, :S]
+        tre_part = parts[:, S:]
+        nc.scalar.activation(lev_part, lev_sf[:], ACT.Copy, scale=lev_gain[:])
+        nc.scalar.activation(tre_part, tre_sf[:], ACT.Copy, scale=tre_gain[:])
         w_codes = keep.tile([P, PASSES * M], U32, name="w_codes", align_bytes=64)
         w_scale = keep.tile([P, PASSES * M], U8, name="w_scale", align_bytes=64)
         nc.vector.quantize_mx(out=w_codes[:].bitcast(FP8X4), scales=w_scale[:],
@@ -89,13 +108,12 @@ def tile_picked_yholtw_fc_p_kernel(tc, x_words, x_scales, w1, lev, tre, seas, al
             nc.vector.tensor_copy(x_codes[1][:, cols[h]],
                                   word_win[1][:].bitcast(U32).indirect(obs_list[:, h * HALF // 16 : (h + 1) * HALF // 16]))
 
-        gain = keep.tile([P, 1], F32, name="gain")
-        nc.scalar.mul(gain[:], alpha_col[:], 1.0 + 1.7 * 0.2)
-
         pred_sf = keep.tile([P, S], F32, name="pred_sf")
-        nc.vector.scalar_tensor_tensor(pred_sf[:], tre_sf[:], 0.9, lev_sf[:], ALU.mult, ALU.add)
         base = keep.tile([P, S], F32, name="base")
-        nc.vector.scalar_tensor_tensor(base[:], tre_sf[:], 0.9 + 1.7 * 0.9, lev_sf[:], ALU.mult, ALU.add)
+        for h in range(HALVES):
+            nc.gpsimd.tensor_tensor(pred_sf[:, cols[h]], lev_sf[:, cols[h]], tre_sf[:, cols[h]], ALU.add)
+        for h in range(HALVES):
+            nc.gpsimd.tensor_tensor(base[:, cols[h]], lev_part[:, cols[h]], tre_part[:, cols[h]], ALU.add)
 
         y = [psum.tile([P, HALF], F32, name="y%d" % h) for h in range(HALVES)]
         for o in range(PASSES):
@@ -118,8 +136,7 @@ def tile_picked_yholtw_fc_p_kernel(tc, x_words, x_scales, w1, lev, tre, seas, al
         for h in range(HALVES):
             nc.vector.tensor_tensor(miss[h][:], y[h][:], pred_sf[:, cols[h]], ALU.subtract)
             nc.scalar.activation(size[h][:], miss[h][:], ACT.Abs)
-        for h in range(HALVES):
-            nc.vector.scalar_tensor_tensor(fore[h][:], miss[h][:], gain[:], base[:, cols[h]], ALU.mult, ALU.add)
+            nc.vector.scalar_tensor_tensor(fore[h][:], y[h][:], gain[:], base[:, cols[h]], ALU.mult, ALU.add)
         for h in range(HALVES):
             nc.vector.tensor_tensor(abs_err[h][:], size[h][:], inv_abs[:, cols[h]], ALU.mult)
         for h in range(HALVES):

@@ -42,7 +42,7 @@ def tile_picked_yholtw_fc_p_kernel(tc, x_words, x_scales, w1, lev, tre, seas, al
         w_raw = [keep.tile([P, PACK, M], F32, name="w_raw%d" % o, tag="w_raw%d" % o) for o in range(PASSES)]
         alpha_col = keep.tile([P, 1], F32, name="alpha_col")
 
-        nc.vector.memset(scale_win[:].bitcast(I32), 0)
+        nc.gpsimd.memset(scale_win[:].bitcast(I32), 0)
         nc.vector.memset(seas_win[:, R:], 0.0)
 
         nc.sync.dma_start(sea_list[:], sea)
@@ -50,12 +50,12 @@ def tile_picked_yholtw_fc_p_kernel(tc, x_words, x_scales, w1, lev, tre, seas, al
         nc.sync.dma_start(ser_list[:], ser)
         nc.sync.dma_start(lev_win[:], lev)
         nc.sync.dma_start(tre_win[:], tre)
-        nc.sync.dma_start(alpha_col[:], alpha)
         nc.sync.dma_start(obs_list[:], offs)
         nc.sync.dma_start(word_win[0][:], x_words[0].rearrange("p c r -> p (c r)").bitcast(I32))
-        for q in range(4):
-            nc.sync.dma_start(scale_win[32 * q : 32 * q + 4 * PASSES, :].bitcast(I32),
-                              x_scales[:, 4 * q : 4 * q + 4, :].bitcast(I32))
+        for q, queue in enumerate([nc.gpsimd, nc.gpsimd, nc.sync, nc.sync]):
+            queue.dma_start(scale_win[32 * q : 32 * q + 4 * PASSES, :].bitcast(I32),
+                            x_scales[:, 4 * q : 4 * q + 4, :].bitcast(I32))
+        nc.sync.dma_start(alpha_col[:], alpha)
         for o in range(PASSES):
             nc.sync.dma_start(w_raw[o][:], w1[o * K_PASS : (o + 1) * K_PASS, :].rearrange("(p j) m -> p j m", j=PACK))
         nc.sync.dma_start(word_win[1][:], x_words[1].rearrange("p c r -> p (c r)").bitcast(I32))
@@ -66,13 +66,6 @@ def tile_picked_yholtw_fc_p_kernel(tc, x_words, x_scales, w1, lev, tre, seas, al
         nc.vector.tensor_copy(lev_g[:], lev_win[:].indirect(ser_list[:]))
         tre_g = keep.tile([P, S], F32, name="tre_g")
         nc.vector.tensor_copy(tre_g[:], tre_win[:].indirect(ser_list[:]))
-
-        gain = keep.tile([P, 1], F32, name="gain")
-        lev_gain = keep.tile([P, 1], F32, name="lev_gain")
-        tre_gain = keep.tile([P, 1], F32, name="tre_gain")
-        nc.gpsimd.tensor_scalar(gain[:], alpha_col[:], GAIN, 0.0, ALU.mult, ALU.add)
-        nc.gpsimd.tensor_scalar(lev_gain[:], alpha_col[:], -GAIN, 1.0, ALU.mult, ALU.add)
-        nc.gpsimd.tensor_scalar(tre_gain[:], alpha_col[:], -GAIN, 1.0 + 1.7, ALU.mult, ALU.add)
 
         inv_root = keep.tile([P, S], F32, name="inv_root")
         nc.scalar.activation(inv_root[:], sf[:], ACT.Abs_reciprocal_sqrt)
@@ -90,9 +83,15 @@ def tile_picked_yholtw_fc_p_kernel(tc, x_words, x_scales, w1, lev, tre, seas, al
         x_scale = keep.tile([P, S], U8, name="x_scale", align_bytes=64)
         nc.vector.tensor_copy(x_scale[:], scale_win[:].indirect(obs_list[:]))
 
-        w_bf = keep.tile([P, PASSES, M, PACK], BF16, name="w_bf", align_bytes=64)
+        w_bf = keep.tile([P, PASSES, M, PACK], BF16, name="w_bf", tag="w_bf", align_bytes=64)
         for o in range(PASSES):
             nc.scalar.copy(w_bf[:, o, :, :], w_raw[o][:].rearrange("p j m -> p m j"))
+        gain = keep.tile([P, 1], F32, name="gain")
+        lev_gain = keep.tile([P, 1], F32, name="lev_gain")
+        tre_gain = keep.tile([P, 1], F32, name="tre_gain")
+        nc.scalar.activation(gain[:], alpha_col[:], ACT.Copy, scale=GAIN)
+        nc.scalar.activation(lev_gain[:], alpha_col[:], ACT.Copy, scale=-GAIN, bias=1.0)
+        nc.scalar.activation(tre_gain[:], alpha_col[:], ACT.Copy, scale=-GAIN, bias=1.0 + 1.7)
         parts = keep.tile([P, 2 * S], F32, name="parts", tag="w_raw1")
         lev_part = parts[:, :S]
         tre_part = parts[:, S:]
@@ -108,12 +107,14 @@ def tile_picked_yholtw_fc_p_kernel(tc, x_words, x_scales, w1, lev, tre, seas, al
             nc.vector.tensor_copy(x_codes[1][:, cols[h]],
                                   word_win[1][:].bitcast(U32).indirect(obs_list[:, h * HALF // 16 : (h + 1) * HALF // 16]))
 
-        pred_sf = keep.tile([P, S], F32, name="pred_sf")
-        base = keep.tile([P, S], F32, name="base")
-        for h in range(HALVES):
-            nc.gpsimd.tensor_tensor(pred_sf[:, cols[h]], lev_sf[:, cols[h]], tre_sf[:, cols[h]], ALU.add)
-        for h in range(HALVES):
-            nc.gpsimd.tensor_tensor(base[:, cols[h]], lev_part[:, cols[h]], tre_part[:, cols[h]], ALU.add)
+        pred_first = keep.tile([P, HALF], F32, name="pred_first")
+        late = keep.tile([P, 3 * HALF], F32, name="late", tag="w_bf", align_bytes=64)
+        pred_sf = [pred_first[:], late[:, :HALF]]
+        base = [late[:, HALF : 2 * HALF], late[:, 2 * HALF :]]
+        nc.gpsimd.tensor_tensor(pred_sf[0], lev_sf[:, cols[0]], tre_sf[:, cols[0]], ALU.add)
+        nc.gpsimd.tensor_tensor(base[0], lev_part[:, cols[0]], tre_part[:, cols[0]], ALU.add)
+        nc.gpsimd.tensor_tensor(pred_sf[1], lev_sf[:, cols[1]], tre_sf[:, cols[1]], ALU.add)
+        nc.gpsimd.tensor_tensor(base[1], lev_part[:, cols[1]], tre_part[:, cols[1]], ALU.add)
 
         y = [psum.tile([P, HALF], F32, name="y%d" % h) for h in range(HALVES)]
         for o in range(PASSES):
@@ -134,9 +135,9 @@ def tile_picked_yholtw_fc_p_kernel(tc, x_words, x_scales, w1, lev, tre, seas, al
         abs_err = [keep.tile([P, HALF], F32, name="abs_err%d" % h) for h in range(HALVES)]
         result = [keep.tile([P, HALF], F32, name="result%d" % h) for h in range(HALVES)]
         for h in range(HALVES):
-            nc.vector.tensor_tensor(miss[h][:], y[h][:], pred_sf[:, cols[h]], ALU.subtract)
+            nc.vector.tensor_tensor(miss[h][:], y[h][:], pred_sf[h], ALU.subtract)
             nc.scalar.activation(size[h][:], miss[h][:], ACT.Abs)
-            nc.vector.scalar_tensor_tensor(fore[h][:], y[h][:], gain[:], base[:, cols[h]], ALU.mult, ALU.add)
+            nc.vector.scalar_tensor_tensor(fore[h][:], y[h][:], gain[:], base[h], ALU.mult, ALU.add)
         for h in range(HALVES):
             nc.vector.tensor_tensor(abs_err[h][:], size[h][:], inv_abs[:, cols[h]], ALU.mult)
         for h in range(HALVES):

from contextlib import ExitStack

import concourse.mybir as mybir

K, T, S, M, U, R = 1024, 1024, 512, 128, 1024, 256
FLOPS = 2 * K * M * S

F32 = mybir.dt.float32
BF16 = mybir.dt.bfloat16
I32 = mybir.dt.int32
U32 = mybir.dt.uint32
U16 = mybir.dt.uint16
U8 = mybir.dt.uint8
FP8X4 = mybir.dt.float8_e4m3fn_x4
ACT = mybir.ActivationFunctionType
ALU = mybir.AluOpType

P = 128
PACK = 4
K_PASS = P * PACK
PASSES = K // K_PASS
SEAS_WINDOW = 704
GAIN = 1.0 + 1.7 * 0.2
HALVES = 2
HALF = S // HALVES


def tile_picked_yholtw_fc_p_kernel(tc, x_words, x_scales, w1, lev, tre, seas, alpha, offs, ser, sea, out):
    nc = tc.nc
    with ExitStack() as ctx:
        keep = ctx.enter_context(tc.tile_pool(name="keep", bufs=1))
        psum = ctx.enter_context(tc.psum_pool(name="psum", bufs=1))

        sea_list = keep.tile([P, S // 16], U16, name="sea_list")
        ser_list = keep.tile([P, S // 16], U16, name="ser_list")
        obs_list = keep.tile([P, S // 16], U16, name="obs_list")
        seas_win = keep.tile([P, SEAS_WINDOW], F32, name="seas_win")
        lev_win = keep.tile([P, U], F32, name="lev_win")
        tre_win = keep.tile([P, U], F32, name="tre_win")
        word_win = [keep.tile([P, T], I32, name="word_win%d" % o) for o in range(PASSES)]
        scale_win = keep.tile([P, T], U8, name="scale_win")
        w_raw = [keep.tile([P, PACK, M], F32, name="w_raw%d" % o, tag="w_raw%d" % o) for o in range(PASSES)]
        alpha_col = keep.tile([P, 1], F32, name="alpha_col")

        nc.gpsimd.memset(scale_win[:].bitcast(I32), 0)
        nc.vector.memset(seas_win[:, R:], 0.0)

        nc.sync.dma_start(sea_list[:], sea)
        nc.sync.dma_start(seas_win[:, :R], seas)
        nc.sync.dma_start(ser_list[:], ser)
        nc.sync.dma_start(lev_win[:], lev)
        nc.sync.dma_start(tre_win[:], tre)
        nc.sync.dma_start(obs_list[:], offs)
        nc.sync.dma_start(word_win[0][:], x_words[0].rearrange("p c r -> p (c r)").bitcast(I32))
        for q, queue in enumerate([nc.gpsimd, nc.gpsimd, nc.sync, nc.sync]):
            queue.dma_start(scale_win[32 * q : 32 * q + 4 * PASSES, :].bitcast(I32),
                            x_scales[:, 4 * q : 4 * q + 4, :].bitcast(I32))
        nc.sync.dma_start(alpha_col[:], alpha)
        for o in range(PASSES):
            nc.sync.dma_start(w_raw[o][:], w1[o * K_PASS : (o + 1) * K_PASS, :].rearrange("(p j) m -> p j m", j=PACK))
        nc.sync.dma_start(word_win[1][:], x_words[1].rearrange("p c r -> p (c r)").bitcast(I32))

        sf = keep.tile([P, S], F32, name="sf")
        nc.vector.tensor_copy(sf[:], seas_win[:].indirect(sea_list[:]))
        lev_g = keep.tile([P, S], F32, name="lev_g")
        nc.vector.tensor_copy(lev_g[:], lev_win[:].indirect(ser_list[:]))
        tre_g = keep.tile([P, S], F32, name="tre_g")
        nc.vector.tensor_copy(tre_g[:], tre_win[:].indirect(ser_list[:]))

        inv_root = keep.tile([P, S], F32, name="inv_root")
        nc.scalar.activation(inv_root[:], sf[:], ACT.Abs_reciprocal_sqrt)
        damped_sf = keep.tile([P, S], F32, name="damped_sf")
        nc.scalar.mul(damped_sf[:], sf[:], 0.9)
        lev_sf = keep.tile([P, S], F32, name="lev_sf")
        nc.gpsimd.tensor_tensor(lev_sf[:], lev_g[:], sf[:], ALU.mult)
        tre_sf = keep.tile([P, S], F32, name="tre_sf")
        nc.gpsimd.tensor_tensor(tre_sf[:], tre_g[:], damped_sf[:], ALU.mult)
        inv_abs = keep.tile([P, S], F32, name="inv_abs")
        nc.scalar.activation(inv_abs[:], inv_root[:], ACT.Square)

        x_codes = [keep.tile([P, S], U32, name="x_codes%d" % o, align_bytes=64) for o in range(PASSES)]
        nc.vector.tensor_copy(x_codes[0][:], word_win[0][:].bitcast(U32).indirect(obs_list[:]))
        x_scale = keep.tile([P, S], U8, name="x_scale", align_bytes=64)
        nc.vector.tensor_copy(x_scale[:], scale_win[:].indirect(obs_list[:]))

        w_bf = keep.tile([P, PASSES, M, PACK], BF16, name="w_bf", tag="w_bf", align_bytes=64)
        for o in range(PASSES):
            nc.scalar.copy(w_bf[:, o, :, :], w_raw[o][:].rearrange("p j m -> p m j"))
        gain = keep.tile([P, 1], F32, name="gain")
        lev_gain = keep.tile([P, 1], F32, name="lev_gain")
        tre_gain = keep.tile([P, 1], F32, name="tre_gain")
        nc.scalar.activation(gain[:], alpha_col[:], ACT.Copy, scale=GAIN)
        nc.scalar.activation(lev_gain[:], alpha_col[:], ACT.Copy, scale=-GAIN, bias=1.0)
        nc.scalar.activation(tre_gain[:], alpha_col[:], ACT.Copy, scale=-GAIN, bias=1.0 + 1.7)
        parts = keep.tile([P, 2 * S], F32, name="parts", tag="w_raw1")
        lev_part = parts[:, :S]
        tre_part = parts[:, S:]
        nc.scalar.activation(lev_part, lev_sf[:], ACT.Copy, scale=lev_gain[:])
        nc.scalar.activation(tre_part, tre_sf[:], ACT.Copy, scale=tre_gain[:])
        w_codes = keep.tile([P, PASSES * M], U32, name="w_codes", align_bytes=64)
        w_scale = keep.tile([P, PASSES * M], U8, name="w_scale", align_bytes=64)
        nc.vector.quantize_mx(out=w_codes[:].bitcast(FP8X4), scales=w_scale[:],
                              in_=w_bf[:].rearrange("p o m j -> p (o m j)"))

        cols = [slice(h * HALF, (h + 1) * HALF) for h in range(HALVES)]
        for h in range(HALVES):
            nc.vector.tensor_copy(x_codes[1][:, cols[h]],
                                  word_win[1][:].bitcast(U32).indirect(obs_list[:, h * HALF // 16 : (h + 1) * HALF // 16]))

        pred_first = keep.tile([P, HALF], F32, name="pred_first")
        late = keep.tile([P, 3 * HALF], F32, name="late", tag="w_bf", align_bytes=64)
        pred_sf = [pred_first[:], late[:, :HALF]]
        base = [late[:, HALF : 2 * HALF], late[:, 2 * HALF :]]
        nc.gpsimd.tensor_tensor(pred_sf[0], lev_sf[:, cols[0]], tre_sf[:, cols[0]], ALU.add)
        nc.gpsimd.tensor_tensor(base[0], lev_part[:, cols[0]], tre_part[:, cols[0]], ALU.add)
        nc.gpsimd.tensor_tensor(pred_sf[1], lev_sf[:, cols[1]], tre_sf[:, cols[1]], ALU.add)
        nc.gpsimd.tensor_tensor(base[1], lev_part[:, cols[1]], tre_part[:, cols[1]], ALU.add)

        y = [psum.tile([P, HALF], F32, name="y%d" % h) for h in range(HALVES)]
        for o in range(PASSES):
            for h in range(HALVES):
                nc.tensor.matmul_mx(
                    out=y[h][:],
                    lhsT=w_codes[:, o * M : (o + 1) * M].bitcast(FP8X4),
                    lhsT_scale=w_scale[:, o * M : (o + 1) * M],
                    rhs=x_codes[o][:, cols[h]].bitcast(FP8X4),
                    rhs_scale=x_scale[4 * o :, cols[h]],
                    start=(o == 0),
                    stop=(o == PASSES - 1),
                )

        miss = [keep.tile([P, HALF], F32, name="miss%d" % h) for h in range(HALVES)]
        size = [keep.tile([P, HALF], F32, name="size%d" % h) for h in range(HALVES)]
        fore = [keep.tile([P, HALF], F32, name="fore%d" % h) for h in range(HALVES)]
        abs_err = [keep.tile([P, HALF], F32, name="abs_err%d" % h) for h in range(HALVES)]
        result = [keep.tile([P, HALF], F32, name="result%d" % h) for h in range(HALVES)]
        for h in range(HALVES):
            nc.vector.tensor_tensor(miss[h][:], y[h][:], pred_sf[h], ALU.subtract)
            nc.scalar.activation(size[h][:], miss[h][:], ACT.Abs)
            nc.vector.scalar_tensor_tensor(fore[h][:], y[h][:], gain[:], base[h], ALU.mult, ALU.add)
        for h in range(HALVES):
            nc.vector.tensor_tensor(abs_err[h][:], size[h][:], inv_abs[:, cols[h]], ALU.mult)
        for h in range(HALVES):
            nc.vector.tensor_tensor(result[h][:], fore[h][:], abs_err[h][:], ALU.subtract)
            nc.sync.dma_start(out[:, cols[h]], result[h][:])
